import numpy as np
import ml_dtypes


def mxq(x, axis, fmt="e4m3"):
    dtype, down = {"e4m3": (ml_dtypes.float8_e4m3fn, 7), "e5m2": (ml_dtypes.float8_e5m2, 14)}[fmt]
    v = np.moveaxis(np.asarray(x, np.float32).astype(ml_dtypes.bfloat16).astype(np.float64), axis, -1)
    blocks = v.reshape(v.shape[:-1] + (-1, 32))
    amax = np.abs(blocks).max(-1, keepdims=True)
    byte = np.maximum(np.where(amax > 0, np.frexp(amax)[1] - 1 + 127, 0) - down, 1)
    scale = np.exp2(byte - 127.0)
    codes = (blocks / scale).astype(np.float32).astype(dtype).astype(np.float64)
    return np.moveaxis((codes * scale).reshape(v.shape), -1, axis)


WIDE = False


def mx_kscale(k):
    if not WIDE:
        return np.ones(k)
    levels = np.array([10, -10, 5, -5, 0])
    if k % 512:
        return np.exp2(np.random.permutation(np.resize(levels, k // 32))).repeat(32)
    a = np.empty((k // 512, 16))
    for p in range(k // 512):
        a[p, :8] = np.random.permutation(np.resize(levels, 8))
        for g in range(8):
            far = levels[np.abs(levels - a[p, g]) >= 10]
            a[p, g + 8] = far[np.random.randint(len(far))]
    return np.exp2(a.ravel()).repeat(32)


def f64(x):
    return np.asarray(x).astype(np.float64)


def striped(idx):
    return np.tile(idx.reshape(-1, 16).T, (8, 1)).astype(np.uint16)


def unstriped(offs):
    return offs[:16].T.reshape(-1).astype(np.int64)


def striped8(idx):
    return np.concatenate([x.reshape(-1, 16).T for x in idx]).astype(np.uint16)


def runs(offs, k):
    lists = np.stack([offs[16 * r : 16 * r + 16].T.reshape(-1) for r in range(8)]).astype(np.int64)
    return lists[np.arange(k) % 512 // 64]


def pack_weight(w):
    k, n = w.shape
    w = f64(np.asarray(w, np.float32).astype(ml_dtypes.bfloat16)).reshape(k // 32, 32, n)
    amax = np.abs(w).max(1)
    byte = np.clip(np.where(amax > 0, np.frexp(amax)[1] - 1 + 127 - 7, 1), 1, 254)
    scaled = (w * np.exp2(127.0 - byte)[:, None, :]).reshape(k, n).astype(np.float32)
    words = np.ascontiguousarray(scaled.reshape(k // 512, 128, 4, n).transpose(0, 1, 3, 2)).astype(ml_dtypes.float8_e4m3fn).view(np.uint8)
    return words, np.ascontiguousarray(byte.astype(np.uint8).reshape(k // 512, 16, n))


def unpack_weight(words, scales):
    g, p, n, _ = words.shape
    vals = np.ascontiguousarray(words).view(ml_dtypes.float8_e4m3fn).astype(np.float64) * np.repeat(np.exp2(scales.astype(np.float64) - 127.0), 8, axis=1)[..., None]
    return vals.transpose(0, 1, 3, 2).reshape(g * 512, n)


def sigmoid(v):
    return 1.0 / (1.0 + np.exp(-np.maximum(v, -700.0)))


K, T, S, H, W = 512, 2048, 512, 512, 256


def setup_inputs():
    n = np.random.standard_normal
    s = mx_kscale(K)[:, None]
    u = mx_kscale(H)
    packed_xT = pack_weight(n((K, T)) * s)
    perm = np.stack([np.random.permutation(S) for _ in range(8)])
    perm2 = np.stack([np.random.permutation(S) for _ in range(8)])
    return {
        "x_words": packed_xT[0],
        "x_scales": packed_xT[1],
        "w1": (n((K, H)) / np.sqrt(K) / s).astype(np.float32),
        "gn": (np.random.uniform(0.5, 1.5, (H, 1)) * u[:, None]).astype(np.float32),
        "w2": (n((H, H)) / np.sqrt(H) / u[:, None]).astype(np.float32),
        "offs": striped(np.random.permutation(T)[:S]),
        "n1": striped8(perm[:, :W]),
        "n2": striped8(perm[:, W:]),
        "n3": striped8(perm2[:, :W]),
        "n4": striped8(perm2[:, W:]),
        "n5": striped(np.random.permutation(S)),
        "n6": striped(np.random.permutation(S)),
        "n7": striped(np.random.permutation(S)),
        "n8": striped(np.random.permutation(S)),
    }


def reference(x_words, x_scales, w1, gn, w2, offs, n1, n2, n3, n4, n5, n6, n7, n8):
    xq = unpack_weight(x_words, x_scales)[:, unstriped(offs)]
    y = mxq(f64(w1), 0, "e4m3").T @ xq
    pa = y[np.arange(H)[:, None], runs(n1, H)]
    pb = y[np.arange(H)[:, None], runs(n2, H)]
    rb = np.minimum(pa, pb)
    ra = np.maximum(pa, pb)
    ds = np.zeros((H, S))
    ds[np.arange(H)[:, None], runs(n1, H)] = ra
    dt = ds.copy()
    dt[np.arange(H)[:, None], runs(n2, H)] = rb
    z = f64(gn) * dt
    w2q = mxq(f64(w2), 0, "e4m3")
    a = w2q.T @ mxq(z, 0, "e4m3")
    pb2 = y[np.arange(H)[:, None], runs(n4, H)]
    pa2 = y[np.arange(H)[:, None], runs(n3, H)]
    rb2 = pb2 * sigmoid(pb2 - pa2)
    ra2 = pa2 * sigmoid(pa2 - pb2)
    ds2 = np.zeros((H, S))
    ds2[np.arange(H)[:, None], runs(n3, H)] = ra2
    dt2 = ds2.copy()
    dt2[np.arange(H)[:, None], runs(n4, H)] = rb2
    z2 = f64(gn) * dt2
    b = w2q.T @ mxq(z2, 0, "e4m3")
    return np.maximum(a[:, unstriped(n5)] + b[:, unstriped(n7)], a[:, unstriped(n6)] + b[:, unstriped(n8)])

@@ -1,0 +1,268 @@
+from contextlib import ExitStack
+
+import concourse.mybir as mybir
+
+K, T, S, H, W = 512, 2048, 512, 512, 256
+FLOPS = 3 * 2 * 512 * 512 * 512
+
+F32 = mybir.dt.float32
+BF16 = mybir.dt.bfloat16
+I32 = mybir.dt.int32
+U32 = mybir.dt.uint32
+U16 = mybir.dt.uint16
+U8 = mybir.dt.uint8
+FP8X4 = mybir.dt.float8_e4m3fn_x4
+ALU = mybir.AluOpType
+ACT = mybir.ActivationFunctionType
+
+P = 128
+PACK = 4
+HALF = 256
+
+
+def tile_picked_tiepathborderduel_none_p_kernel(
+    tc, x_words, x_scales, w1, gn, w2, offs, n1, n2, n3, n4, n5, n6, n7, n8, out
+):
+    nc = tc.nc
+    with ExitStack() as ctx:
+        lists = ctx.enter_context(tc.tile_pool(name="lists", bufs=1))
+        keep = ctx.enter_context(tc.tile_pool(name="keep", bufs=1))
+        psum = ctx.enter_context(tc.psum_pool(name="psum", bufs=1))
+
+        def load_list(name, src):
+            t = lists.tile(list(src.shape), U16, name=name)
+            nc.sync.dma_start(t[:], src)
+            return t
+
+        def f32_tiles(name, width):
+            return [keep.tile([P, width], F32, name=f"{name}{t}") for t in range(PACK)]
+
+        l_offs = load_list("l_offs", offs)
+        xs_all = keep.tile([P, T], U8, name="xs_all")
+        nc.vector.memset(xs_all[:].bitcast(I32), 0)
+        for q in range(4):
+            nc.sync.dma_start(xs_all[32 * q : 32 * q + 4, :].bitcast(I32), x_scales[0, 4 * q : 4 * q + 4, :].bitcast(I32))
+        w1_rows = w1.rearrange("(p j) c -> p j c", j=PACK)
+        w1_raw = [keep.tile([P, PACK, HALF], F32, name=f"w1_raw{h}") for h in range(2)]
+        for h in range(2):
+            nc.sync.dma_start(w1_raw[h][:], w1_rows[:, :, h * HALF : (h + 1) * HALF])
+        xw_all = keep.tile([P, T], I32, name="xw_all")
+        nc.sync.dma_start(xw_all[:], x_words[0].rearrange("p n t -> p (n t)").bitcast(I32))
+        l1 = load_list("l1", n1)
+        l2 = load_list("l2", n2)
+        w2_raw = keep.tile([P, PACK, H], F32, name="w2_raw")
+        nc.sync.dma_start(w2_raw[:], w2.rearrange("(p j) c -> p j c", j=PACK))
+        gain = keep.tile([P, PACK], F32, name="gain")
+        nc.sync.dma_start(gain[:], gn.rearrange("(p t) o -> p (t o)", t=PACK))
+        l3 = load_list("l3", n3)
+        l4 = load_list("l4", n4)
+        l5 = load_list("l5", n5)
+        l6 = load_list("l6", n6)
+        l7 = load_list("l7", n7)
+        l8 = load_list("l8", n8)
+
+        def halves(lst):
+            return [(slice(h * HALF, (h + 1) * HALF), lst[:, 16 * h : 16 * (h + 1)]) for h in range(2)]
+
+        half_cols = [slice(0, HALF), slice(HALF, S)]
+
+        w1_g = keep.tile([P, PACK, P, PACK], BF16, name="w1_g", align_bytes=64)
+        xs = keep.tile([P, S], U8, name="xs", align_bytes=64)
+        for h in range(2):
+            dst = w1_g[:, :, 64 * h : 64 * (h + 1), :].rearrange("p t m j -> p m t j")
+            src = w1_raw[h][:].rearrange("p j (m t) -> p m t j", t=PACK)
+            if h == 0:
+                nc.scalar.copy(dst, src)
+                nc.vector.tensor_copy(xs[:], xs_all[:].indirect(l_offs[:]))
+            else:
+                nc.vector.tensor_copy(dst, src)
+        w1_c = keep.tile([P, H], U32, name="w1_c", align_bytes=64)
+        w1_s = keep.tile([P, H], U8, name="w1_s", align_bytes=64)
+        nc.vector.quantize_mx(out=w1_c[:].bitcast(FP8X4), scales=w1_s[:], in_=w1_g[:].rearrange("p t m j -> p (t m j)"))
+
+        xw = keep.tile([P, S], U32, name="xw", align_bytes=64)
+        for cols, part in halves(l_offs):
+            nc.vector.tensor_copy(xw[:, cols], xw_all[:].bitcast(U32).indirect(part))
+
+        def mm(bank, t, w_c, w_s, r_c, r_s, cols):
+            rows = slice(t * P, (t + 1) * P)
+            nc.tensor.matmul_mx(out=bank, lhsT=w_c[:, rows].bitcast(FP8X4), lhsT_scale=w_s[:, rows],
+                                rhs=r_c[:, cols].bitcast(FP8X4), rhs_scale=r_s[:, cols], start=True, stop=True)
+
+        def bank(i, width=S):
+            return psum.tile([P, width], F32, name=f"bank{i}")
+
+        y0_ps = [bank(0, HALF), bank(4, HALF)]
+        y_ps = [None] + [bank(t) for t in range(1, PACK)]
+        for h in range(2):
+            mm(y0_ps[h][:], 0, w1_c, w1_s, xw, xs, half_cols[h])
+        for t in range(1, PACK):
+            mm(y_ps[t][:], t, w1_c, w1_s, xw, xs, slice(0, S))
+
+        def woven(dst, src, cols):
+            return (dst[:, cols, :].rearrange("p (c i) t -> p c t i", i=4), src[:, :, cols].rearrange("p t (c i) -> p c t i", i=4))
+
+        def codes(name):
+            return (keep.tile([P, S], U32, name=f"{name}_c", align_bytes=64), keep.tile([P, S], U8, name=f"{name}_s", align_bytes=64))
+
+        def quantize(c, s, grouped, cols):
+            nc.vector.quantize_mx(out=c[:, cols].bitcast(FP8X4), scales=s[:, cols], in_=grouped[:, cols, :].rearrange("p c t -> p (c t)"))
+
+        def pair_tiles(name):
+            return [keep.tile([P, 2, W], F32, name=f"{name}{u}") for u in range(2)]
+
+        def of(pairs, t):
+            return pairs[t // 2][:, t % 2, :]
+
+        def both(pairs, u):
+            return pairs[u][:].rearrange("p a w -> p (a w)")
+
+        y = f32_tiles("y", S)
+        pa, pb, ra, rb = pair_tiles("pa"), pair_tiles("pb"), pair_tiles("ra"), pair_tiles("rb")
+        dt = f32_tiles("dt", S)
+        pa2, pb2, diff, sa, sb = pair_tiles("pa2"), pair_tiles("pb2"), pair_tiles("diff"), pair_tiles("sa"), pair_tiles("sb")
+        z_pl = keep.tile([P, PACK, S], BF16, name="z_pl", tag="reused2")
+        z2_pl = keep.tile([P, PACK, S], BF16, name="z2_pl")
+
+        def s_gather(dst, window, lst):
+            nc.scalar.activation(dst, window[:].indirect(lst), ACT.Copy)
+
+        def fetch1(t):
+            nc.scalar.copy(y[t][:], y_ps[t][:])
+            s_gather(of(pa, t), y[t], l1[:])
+            s_gather(of(pb, t), y[t], l2[:])
+
+        def put(window, lst, values):
+            nc.vector.tensor_copy(window[:].indirect(lst[:]), values)
+
+        def put_mul(window, lst, values, factor):
+            nc.vector.tensor_tensor(window[:].indirect(lst[:]), values, factor, ALU.mult)
+
+        def fetch2(t):
+            s_gather(of(pa2, t), y[t], l3[:])
+            s_gather(of(pb2, t), y[t], l4[:])
+
+        def sub2(u):
+            nc.vector.tensor_tensor(both(diff, u), both(pa2, u), both(pb2, u), ALU.subtract)
+
+        def gates(u):
+            nc.scalar.activation(both(sa, u), both(diff, u), ACT.Sigmoid)
+            nc.scalar.activation(both(sb, u), both(diff, u), ACT.Sigmoid, scale=-1.0)
+
+        def s_cast(planes, src, t, cols=slice(0, S)):
+            nc.scalar.activation(planes[:, t, cols], src[t][:, cols], ACT.Copy, scale=gain[:, t : t + 1])
+
+        def v_cast(planes, src, t, cols=slice(0, S)):
+            nc.vector.tensor_scalar(planes[:, t, cols], src[t][:, cols], gain[:, t : t + 1], None, ALU.mult)
+
+        nc.scalar.copy(y[0][:, half_cols[0]], y0_ps[0][:])
+        nc.vector.tensor_copy(y[0][:, half_cols[1]], y0_ps[1][:])
+        s_gather(of(pa, 0), y[0], l1[:])
+        nc.vector.tensor_copy(of(pb, 0), y[0][:].indirect(l2[:]))
+        nc.vector.tensor_tensor(of(ra, 0), of(pa, 0), of(pb, 0), ALU.max)
+        put(dt[0], l1, of(ra, 0))
+        fetch1(1)
+        nc.vector.tensor_tensor(of(ra, 1), of(pa, 1), of(pb, 1), ALU.max)
+        nc.vector.tensor_tensor(both(rb, 0), both(pa, 0), both(pb, 0), ALU.min)
+        put(dt[1], l1, of(ra, 1))
+        put(dt[0], l2, of(rb, 0))
+        put(dt[1], l2, of(rb, 1))
+        fetch1(2)
+        fetch1(3)
+        nc.vector.tensor_tensor(both(ra, 1), both(pa, 1), both(pb, 1), ALU.max)
+        nc.vector.tensor_tensor(both(rb, 1), both(pa, 1), both(pb, 1), ALU.min)
+        put(dt[2], l1, of(ra, 2))
+        put(dt[3], l1, of(ra, 3))
+        put(dt[2], l2, of(rb, 2))
+        put(dt[3], l2, of(rb, 3))
+        fetch2(0)
+        fetch2(1)
+        sub2(0)
+        w2_g = keep.tile([P, H, PACK], BF16, name="w2_g", align_bytes=64)
+        nc.scalar.copy(*woven(w2_g, w2_raw, slice(0, H)))
+        w2_c, w2_s = codes("w2")
+        quantize(w2_c, w2_s, w2_g, slice(0, H))
+        s_cast(z_pl, dt, 0)
+        s_cast(z_pl, dt, 1)
+        fetch2(2)
+        fetch2(3)
+        gates(0)
+        s_cast(z_pl, dt, 2)
+        z_g = [keep.tile([P, HALF, PACK], BF16, name=f"z_g{h}", tag=f"reused{h}", align_bytes=64) for h in range(2)]
+        z_c, z_s = codes("z")
+
+        def finish(planes, src, grouped, c, s, v_cols):
+            def weave(h, lo, hi):
+                return (grouped[h][:, lo - h * HALF : hi - h * HALF, :].rearrange("p (c i) t -> p c t i", i=4),
+                        planes[:, :, lo:hi].rearrange("p t (c i) -> p c t i", i=4))
+
+            for cols in half_cols:
+                v_cast(planes, src, 3, cols)
+            nc.vector.tensor_copy(*weave(0, 0, HALF))
+            if v_cols < S:
+                nc.scalar.copy(*weave(1, v_cols, S))
+            if v_cols > HALF:
+                nc.vector.tensor_copy(*weave(1, HALF, v_cols))
+            for h, cols in enumerate(half_cols):
+                nc.vector.quantize_mx(out=c[:, cols].bitcast(FP8X4), scales=s[:, cols], in_=grouped[h][:].rearrange("p c t -> p (c t)"))
+
+        finish(z_pl, dt, z_g, z_c, z_s, 384)
+        sub2(1)
+        gates(1)
+        a_ps = [bank(i) for i in (5, 6, 7, 4)]
+        for m in range(PACK):
+            mm(a_ps[m][:], m, w2_c, w2_s, z_c, z_s, slice(0, S))
+
+        a_w = f32_tiles("a_w", S)
+        a5, a6 = f32_tiles("a5", S), f32_tiles("a6", S)
+
+        def fetch_a(m):
+            nc.scalar.copy(a_w[m][:], a_ps[m][:])
+            for dst, lst in ((a5, l5), (a6, l6)):
+                for cols, part in halves(lst):
+                    s_gather(dst[m][:, cols], a_w[m], part)
+
+        dt2 = [keep.tile([P, S], F32, name=f"dt2_{t}", tag=f"reused{t}", align_bytes=64) for t in range(2)]
+        dt2 += [keep.tile([P, S], F32, name="dt2_2", tag="reused2"), keep.tile([P, S], F32, name="dt2_3", tag="dt3")]
+        put_mul(dt2[0], l3, of(pa2, 0), of(sa, 0))
+        put_mul(dt2[1], l3, of(pa2, 1), of(sa, 1))
+        put_mul(dt2[0], l4, of(pb2, 0), of(sb, 0))
+        put_mul(dt2[1], l4, of(pb2, 1), of(sb, 1))
+        put_mul(dt2[2], l3, of(pa2, 2), of(sa, 2))
+        put_mul(dt2[3], l3, of(pa2, 3), of(sa, 3))
+        put_mul(dt2[2], l4, of(pb2, 2), of(sb, 2))
+        put_mul(dt2[3], l4, of(pb2, 3), of(sb, 3))
+        fetch_a(0)
+        fetch_a(1)
+        s_cast(z2_pl, dt2, 0)
+        s_cast(z2_pl, dt2, 1)
+        fetch_a(2)
+        fetch_a(3)
+        v_cast(z2_pl, dt2, 2)
+        z2_g = [keep.tile([P, HALF, PACK], BF16, name=f"z2_g{h}", align_bytes=64) for h in range(2)]
+        z2_c, z2_s = codes("z2")
+        finish(z2_pl, dt2, z2_g, z2_c, z2_s, 384)
+        b0_ps = [bank(0, HALF), bank(5, HALF)]
+        b_ps = [None] + [bank(i) for i in range(1, PACK)]
+        for h in range(2):
+            mm(b0_ps[h][:], 0, w2_c, w2_s, z2_c, z2_s, half_cols[h])
+        for m in range(1, PACK):
+            mm(b_ps[m][:], m, w2_c, w2_s, z2_c, z2_s, slice(0, S))
+
+        b_w = f32_tiles("b_w", S)
+        b7, b8, s1, s2, res = f32_tiles("b7", S), f32_tiles("b8", S), f32_tiles("s1", S), f32_tiles("s2", S), f32_tiles("res", S)
+        nc.scalar.copy(b_w[0][:, half_cols[0]], b0_ps[0][:])
+        nc.vector.tensor_copy(b_w[0][:, half_cols[1]], b0_ps[1][:])
+        for m in range(PACK):
+            if m + 1 < PACK:
+                nc.vector.tensor_copy(b_w[m + 1][:], b_ps[m + 1][:])
+            for h, ((cols, part7), (same, part8)) in enumerate(zip(halves(l7), halves(l8))):
+                s_gather(b8[m][:, cols], b_w[m], part8)
+                if 2 * m + h < 2:
+                    nc.vector.tensor_tensor(s1[m][:, cols], b_w[m][:].indirect(part7), a5[m][:, cols], ALU.add)
+                else:
+                    s_gather(b7[m][:, cols], b_w[m], part7)
+                    nc.vector.tensor_tensor(s1[m][:, cols], b7[m][:, cols], a5[m][:, cols], ALU.add)
+                nc.vector.tensor_tensor(s2[m][:, cols], b8[m][:, cols], a6[m][:, cols], ALU.add)
+                nc.vector.tensor_tensor(res[m][:, cols], s1[m][:, cols], s2[m][:, cols], ALU.max)
+                nc.sync.dma_start(out[m * P : (m + 1) * P, cols], res[m][:, cols])

@@ -18,6 +18,7 @@ ACT = mybir.ActivationFunctionType
 P = 128
 PACK = 4
 HALF = 256
+SPARE = 16
 
 
 def tile_picked_tiepathborderduel_none_p_kernel(
@@ -27,6 +28,7 @@ def tile_picked_tiepathborderduel_none_p_kernel(
     with ExitStack() as ctx:
         lists = ctx.enter_context(tc.tile_pool(name="lists", bufs=1))
         keep = ctx.enter_context(tc.tile_pool(name="keep", bufs=1))
+        shared = ctx.enter_context(tc.tile_pool(name="shared", bufs=1))
         psum = ctx.enter_context(tc.psum_pool(name="psum", bufs=1))
 
         def load_list(name, src):
@@ -69,8 +71,8 @@ def tile_picked_tiepathborderduel_none_p_kernel(
         w1_g = keep.tile([P, PACK, P, PACK], BF16, name="w1_g", align_bytes=64)
         xs = keep.tile([P, S], U8, name="xs", align_bytes=64)
         for h in range(2):
-            dst = w1_g[:, :, 64 * h : 64 * (h + 1), :].rearrange("p t m j -> p m t j")
-            src = w1_raw[h][:].rearrange("p j (m t) -> p m t j", t=PACK)
+            dst = w1_g[:, :, 64 * h : 64 * (h + 1), :].rearrange("p t m j -> p m j t")
+            src = w1_raw[h][:].rearrange("p j (m t) -> p m j t", t=PACK)
             if h == 0:
                 nc.scalar.copy(dst, src)
                 nc.vector.tensor_copy(xs[:], xs_all[:].indirect(l_offs[:]))
@@ -92,11 +94,12 @@ def tile_picked_tiepathborderduel_none_p_kernel(
         def bank(i, width=S):
             return psum.tile([P, width], F32, name=f"bank{i}")
 
-        y0_ps = [bank(0, HALF), bank(4, HALF)]
-        y_ps = [None] + [bank(t) for t in range(1, PACK)]
+        y_half_ps = [[bank(2 * t + h, HALF) for h in range(2)] for t in range(2)]
+        y_ps = {t: bank(2 + t) for t in (2, 3)}
         for h in range(2):
-            mm(y0_ps[h][:], 0, w1_c, w1_s, xw, xs, half_cols[h])
-        for t in range(1, PACK):
+            for t in range(2):
+                mm(y_half_ps[t][h][:], t, w1_c, w1_s, xw, xs, half_cols[h])
+        for t in (2, 3):
             mm(y_ps[t][:], t, w1_c, w1_s, xw, xs, slice(0, S))
 
         def woven(dst, src, cols):
@@ -120,15 +123,13 @@ def tile_picked_tiepathborderduel_none_p_kernel(
         y = f32_tiles("y", S)
         pa, pb, ra, rb = pair_tiles("pa"), pair_tiles("pb"), pair_tiles("ra"), pair_tiles("rb")
         dt = f32_tiles("dt", S)
-        pa2, pb2, diff, sa, sb = pair_tiles("pa2"), pair_tiles("pb2"), pair_tiles("diff"), pair_tiles("sa"), pair_tiles("sb")
-        z_pl = keep.tile([P, PACK, S], BF16, name="z_pl", tag="reused2")
-        z2_pl = keep.tile([P, PACK, S], BF16, name="z2_pl")
+        pa2, pb2, diff, sa = pair_tiles("pa2"), pair_tiles("pb2"), pair_tiles("diff"), pair_tiles("sa")
+        z_pl = keep.tile([P, PACK, S], BF16, name="z_pl")
 
         def s_gather(dst, window, lst):
             nc.scalar.activation(dst, window[:].indirect(lst), ACT.Copy)
 
         def fetch1(t):
-            nc.scalar.copy(y[t][:], y_ps[t][:])
             s_gather(of(pa, t), y[t], l1[:])
             s_gather(of(pb, t), y[t], l2[:])
 
@@ -145,9 +146,8 @@ def tile_picked_tiepathborderduel_none_p_kernel(
         def sub2(u):
             nc.vector.tensor_tensor(both(diff, u), both(pa2, u), both(pb2, u), ALU.subtract)
 
-        def gates(u):
-            nc.scalar.activation(both(sa, u), both(diff, u), ACT.Sigmoid)
-            nc.scalar.activation(both(sb, u), both(diff, u), ACT.Sigmoid, scale=-1.0)
+        def gate(dst, u, sign):
+            nc.scalar.activation(both(dst, u), both(diff, u), ACT.Sigmoid, scale=sign)
 
         def s_cast(planes, src, t, cols=slice(0, S)):
             nc.scalar.activation(planes[:, t, cols], src[t][:, cols], ACT.Copy, scale=gain[:, t : t + 1])
@@ -155,8 +155,10 @@ def tile_picked_tiepathborderduel_none_p_kernel(
         def v_cast(planes, src, t, cols=slice(0, S)):
             nc.vector.tensor_scalar(planes[:, t, cols], src[t][:, cols], gain[:, t : t + 1], None, ALU.mult)
 
-        nc.scalar.copy(y[0][:, half_cols[0]], y0_ps[0][:])
-        nc.vector.tensor_copy(y[0][:, half_cols[1]], y0_ps[1][:])
+        nc.scalar.copy(y[0][:, half_cols[0]], y_half_ps[0][0][:])
+        nc.scalar.copy(y[1][:, half_cols[0]], y_half_ps[1][0][:])
+        nc.vector.tensor_copy(y[0][:, half_cols[1]], y_half_ps[0][1][:])
+        nc.scalar.copy(y[1][:, half_cols[1]], y_half_ps[1][1][:])
         s_gather(of(pa, 0), y[0], l1[:])
         nc.vector.tensor_copy(of(pb, 0), y[0][:].indirect(l2[:]))
         nc.vector.tensor_tensor(of(ra, 0), of(pa, 0), of(pb, 0), ALU.max)
@@ -167,7 +169,12 @@ def tile_picked_tiepathborderduel_none_p_kernel(
         put(dt[1], l1, of(ra, 1))
         put(dt[0], l2, of(rb, 0))
         put(dt[1], l2, of(rb, 1))
+        for t in (2, 3):
+            nc.scalar.copy(y[t][:], y_ps[t][:])
         fetch1(2)
+        fetch2(0)
+        fetch2(1)
+        sub2(0)
         fetch1(3)
         nc.vector.tensor_tensor(both(ra, 1), both(pa, 1), both(pb, 1), ALU.max)
         nc.vector.tensor_tensor(both(rb, 1), both(pa, 1), both(pb, 1), ALU.min)
@@ -175,90 +182,101 @@ def tile_picked_tiepathborderduel_none_p_kernel(
         put(dt[3], l1, of(ra, 3))
         put(dt[2], l2, of(rb, 2))
         put(dt[3], l2, of(rb, 3))
-        fetch2(0)
-        fetch2(1)
-        sub2(0)
         w2_g = keep.tile([P, H, PACK], BF16, name="w2_g", align_bytes=64)
         nc.scalar.copy(*woven(w2_g, w2_raw, slice(0, H)))
-        w2_c, w2_s = codes("w2")
-        quantize(w2_c, w2_s, w2_g, slice(0, H))
         s_cast(z_pl, dt, 0)
         s_cast(z_pl, dt, 1)
         fetch2(2)
         fetch2(3)
-        gates(0)
+        gate(sa, 0, 1.0)
         s_cast(z_pl, dt, 2)
-        z_g = [keep.tile([P, HALF, PACK], BF16, name=f"z_g{h}", tag=f"reused{h}", align_bytes=64) for h in range(2)]
+        sb = pair_tiles("sb")
+        gate(sb, 0, -1.0)
+        z_g = shared.tile([P, S, PACK], BF16, name="z_g", align_bytes=64, offset=0)
         z_c, z_s = codes("z")
-
-        def finish(planes, src, grouped, c, s, v_cols):
-            def weave(h, lo, hi):
-                return (grouped[h][:, lo - h * HALF : hi - h * HALF, :].rearrange("p (c i) t -> p c t i", i=4),
-                        planes[:, :, lo:hi].rearrange("p t (c i) -> p c t i", i=4))
-
-            for cols in half_cols:
-                v_cast(planes, src, 3, cols)
-            nc.vector.tensor_copy(*weave(0, 0, HALF))
-            if v_cols < S:
-                nc.scalar.copy(*weave(1, v_cols, S))
-            if v_cols > HALF:
-                nc.vector.tensor_copy(*weave(1, HALF, v_cols))
-            for h, cols in enumerate(half_cols):
-                nc.vector.quantize_mx(out=c[:, cols].bitcast(FP8X4), scales=s[:, cols], in_=grouped[h][:].rearrange("p c t -> p (c t)"))
-
-        finish(z_pl, dt, z_g, z_c, z_s, 384)
+        v1_cols, s1_cols = slice(0, 256), slice(256, S)
+        v_cast(z_pl, dt, 3)
+        w2_c, w2_s = codes("w2")
+        quantize(w2_c, w2_s, w2_g, slice(0, H))
+        nc.vector.tensor_copy(*woven(z_g, z_pl, v1_cols))
+        nc.scalar.copy(*woven(z_g, z_pl, s1_cols))
         sub2(1)
-        gates(1)
-        a_ps = [bank(i) for i in (5, 6, 7, 4)]
+        quantize(z_c, z_s, z_g, slice(0, S))
+        dt2 = [shared.tile([P, S], F32, name=f"dt2_{t}", align_bytes=64, offset=4 * S * t) for t in range(2)]
+        dt2 += [keep.tile([P, S], F32, name=f"dt2_{t}") for t in (2, 3)]
+        gate(sa, 1, 1.0)
+        gate(sb, 1, -1.0)
+        put_mul(dt2[0], l3, of(pa2, 0), of(sa, 0))
+        put_mul(dt2[1], l3, of(pa2, 1), of(sa, 1))
+        a_ps = [bank(i) for i in (6, 7, 0, 1)]
         for m in range(PACK):
             mm(a_ps[m][:], m, w2_c, w2_s, z_c, z_s, slice(0, S))
 
-        a_w = f32_tiles("a_w", S)
+        def windows(name):
+            tiles = f32_tiles(name, S + SPARE)
+            for t in tiles:
+                nc.gpsimd.memset(t[:, S:], 0.0)
+            return tiles
+
+        a_w, b_w = windows("a_w"), windows("b_w")
         a5, a6 = f32_tiles("a5", S), f32_tiles("a6", S)
 
-        def fetch_a(m):
-            nc.scalar.copy(a_w[m][:], a_ps[m][:])
-            for dst, lst in ((a5, l5), (a6, l6)):
-                for cols, part in halves(lst):
-                    s_gather(dst[m][:, cols], a_w[m], part)
+        def gather_a(m):
+            s_gather(a5[m][:], a_w[m], l5[:])
+            s_gather(a6[m][:], a_w[m], l6[:])
 
-        dt2 = [keep.tile([P, S], F32, name=f"dt2_{t}", tag=f"reused{t}", align_bytes=64) for t in range(2)]
-        dt2 += [keep.tile([P, S], F32, name="dt2_2", tag="reused2"), keep.tile([P, S], F32, name="dt2_3", tag="dt3")]
-        put_mul(dt2[0], l3, of(pa2, 0), of(sa, 0))
-        put_mul(dt2[1], l3, of(pa2, 1), of(sa, 1))
         put_mul(dt2[0], l4, of(pb2, 0), of(sb, 0))
         put_mul(dt2[1], l4, of(pb2, 1), of(sb, 1))
         put_mul(dt2[2], l3, of(pa2, 2), of(sa, 2))
         put_mul(dt2[3], l3, of(pa2, 3), of(sa, 3))
         put_mul(dt2[2], l4, of(pb2, 2), of(sb, 2))
         put_mul(dt2[3], l4, of(pb2, 3), of(sb, 3))
-        fetch_a(0)
-        fetch_a(1)
+
+        def evac_a(m):
+            nc.scalar.copy(a_w[m][:, :S], a_ps[m][:])
+
+        for m in range(PACK):
+            evac_a(m)
+        gather_a(0)
+        gather_a(1)
+        z2_pl = keep.tile([P, PACK, S], BF16, name="z2_pl", tag="a_w1")
         s_cast(z2_pl, dt2, 0)
         s_cast(z2_pl, dt2, 1)
-        fetch_a(2)
-        fetch_a(3)
-        v_cast(z2_pl, dt2, 2)
+        gather_a(2)
+        s_cast(z2_pl, dt2, 2)
+        s_gather(a5[3][:], a_w[3], l5[:])
         z2_g = [keep.tile([P, HALF, PACK], BF16, name=f"z2_g{h}", align_bytes=64) for h in range(2)]
         z2_c, z2_s = codes("z2")
-        finish(z2_pl, dt2, z2_g, z2_c, z2_s, 384)
-        b0_ps = [bank(0, HALF), bank(5, HALF)]
-        b_ps = [None] + [bank(i) for i in range(1, PACK)]
+        for cols in half_cols:
+            v_cast(z2_pl, dt2, 3, cols)
+        def weave(h, lo, hi):
+            return (z2_g[h][:, lo - h * HALF : hi - h * HALF, :].rearrange("p (c i) t -> p c t i", i=4),
+                    z2_pl[:, :, lo:hi].rearrange("p t (c i) -> p c t i", i=4))
+
+        nc.vector.tensor_copy(*weave(0, 0, HALF))
+        nc.scalar.copy(*weave(1, 384, S))
+        nc.vector.tensor_copy(*weave(1, HALF, 384))
+        for h, cols in enumerate(half_cols):
+            nc.vector.quantize_mx(out=z2_c[:, cols].bitcast(FP8X4), scales=z2_s[:, cols], in_=z2_g[h][:].rearrange("p c t -> p (c t)"))
+        s_gather(a6[3][:], a_w[3], l6[:])
+        b0_ps = [bank(2, HALF), bank(3, HALF)]
+        b_ps = [None] + [bank(i) for i in (4, 5, 6)]
         for h in range(2):
             mm(b0_ps[h][:], 0, w2_c, w2_s, z2_c, z2_s, half_cols[h])
         for m in range(1, PACK):
             mm(b_ps[m][:], m, w2_c, w2_s, z2_c, z2_s, slice(0, S))
 
-        b_w = f32_tiles("b_w", S)
         b7, b8, s1, s2, res = f32_tiles("b7", S), f32_tiles("b8", S), f32_tiles("s1", S), f32_tiles("s2", S), f32_tiles("res", S)
         nc.scalar.copy(b_w[0][:, half_cols[0]], b0_ps[0][:])
         nc.vector.tensor_copy(b_w[0][:, half_cols[1]], b0_ps[1][:])
         for m in range(PACK):
             if m + 1 < PACK:
-                nc.vector.tensor_copy(b_w[m + 1][:], b_ps[m + 1][:])
-            for h, ((cols, part7), (same, part8)) in enumerate(zip(halves(l7), halves(l8))):
+                nc.scalar.copy(b_w[m + 1][:, :S], b_ps[m + 1][:])
+            whole = [(slice(0, S), l7[:], l8[:])]
+            parts = [(cols, part7, part8) for (cols, part7), (same, part8) in zip(halves(l7), halves(l8))]
+            for h, (cols, part7, part8) in enumerate(whole if m < PACK - 1 else parts):
                 s_gather(b8[m][:, cols], b_w[m], part8)
-                if 2 * m + h < 2:
+                if m < 3 or (m == PACK - 1 and h < 1):
                     nc.vector.tensor_tensor(s1[m][:, cols], b_w[m][:].indirect(part7), a5[m][:, cols], ALU.add)
                 else:
                     s_gather(b7[m][:, cols], b_w[m], part7)

@@ -39,25 +39,25 @@ def tile_picked_tiepathborderduel_none_p_kernel(
         def f32_tiles(name, width):
             return [keep.tile([P, width], F32, name=f"{name}{t}") for t in range(PACK)]
 
-        l_offs = load_list("l_offs", offs)
-        xs_all = keep.tile([P, T], U8, name="xs_all")
-        nc.vector.memset(xs_all[:].bitcast(I32), 0)
-        for q in range(4):
-            nc.sync.dma_start(xs_all[32 * q : 32 * q + 4, :].bitcast(I32), x_scales[0, 4 * q : 4 * q + 4, :].bitcast(I32))
         w1_rows = w1.rearrange("(p j) c -> p j c", j=PACK)
         w1_raw = [keep.tile([P, PACK, HALF], F32, name=f"w1_raw{h}") for h in range(2)]
-        for h in range(2):
-            nc.sync.dma_start(w1_raw[h][:], w1_rows[:, :, h * HALF : (h + 1) * HALF])
+        nc.sync.dma_start(w1_raw[0][:], w1_rows[:, :, :HALF])
+        l_offs = load_list("l_offs", offs)
+        xs_all = keep.tile([P, T], U8, name="xs_all")
+        nc.gpsimd.memset(xs_all[:].bitcast(I32), 0)
+        for q in range(4):
+            nc.sync.dma_start(xs_all[32 * q : 32 * q + 4, :].bitcast(I32), x_scales[0, 4 * q : 4 * q + 4, :].bitcast(I32))
+        nc.sync.dma_start(w1_raw[1][:], w1_rows[:, :, HALF:])
         xw_all = keep.tile([P, T], I32, name="xw_all")
         nc.sync.dma_start(xw_all[:], x_words[0].rearrange("p n t -> p (n t)").bitcast(I32))
         l1 = load_list("l1", n1)
         l2 = load_list("l2", n2)
+        l3 = load_list("l3", n3)
+        l4 = load_list("l4", n4)
         w2_raw = keep.tile([P, PACK, H], F32, name="w2_raw")
         nc.sync.dma_start(w2_raw[:], w2.rearrange("(p j) c -> p j c", j=PACK))
         gain = keep.tile([P, PACK], F32, name="gain")
         nc.sync.dma_start(gain[:], gn.rearrange("(p t) o -> p (t o)", t=PACK))
-        l3 = load_list("l3", n3)
-        l4 = load_list("l4", n4)
         l5 = load_list("l5", n5)
         l6 = load_list("l6", n6)
         l7 = load_list("l7", n7)
@@ -112,7 +112,7 @@ def tile_picked_tiepathborderduel_none_p_kernel(
             nc.vector.quantize_mx(out=c[:, cols].bitcast(FP8X4), scales=s[:, cols], in_=grouped[:, cols, :].rearrange("p c t -> p (c t)"))
 
         def pair_tiles(name):
-            return [keep.tile([P, 2, W], F32, name=f"{name}{u}") for u in range(2)]
+            return [keep.tile([P, 2, W], F32, name=f"{name}{u}", align_bytes=64) for u in range(2)]
 
         def of(pairs, t):
             return pairs[t // 2][:, t % 2, :]
@@ -144,7 +144,7 @@ def tile_picked_tiepathborderduel_none_p_kernel(
             s_gather(of(pb2, t), y[t], l4[:])
 
         def sub2(u):
-            nc.vector.tensor_tensor(both(diff, u), both(pa2, u), both(pb2, u), ALU.subtract)
+            nc.gpsimd.tensor_tensor(both(diff, u), both(pa2, u), both(pb2, u), ALU.subtract)
 
         def gate(dst, u, sign):
             nc.scalar.activation(both(dst, u), both(diff, u), ACT.Sigmoid, scale=sign)
@@ -171,10 +171,10 @@ def tile_picked_tiepathborderduel_none_p_kernel(
         put(dt[1], l2, of(rb, 1))
         for t in (2, 3):
             nc.scalar.copy(y[t][:], y_ps[t][:])
-        fetch1(2)
         fetch2(0)
         fetch2(1)
         sub2(0)
+        fetch1(2)
         fetch1(3)
         nc.vector.tensor_tensor(both(ra, 1), both(pa, 1), both(pb, 1), ALU.max)
         nc.vector.tensor_tensor(both(rb, 1), both(pa, 1), both(pb, 1), ALU.min)
@@ -182,8 +182,8 @@ def tile_picked_tiepathborderduel_none_p_kernel(
         put(dt[3], l1, of(ra, 3))
         put(dt[2], l2, of(rb, 2))
         put(dt[3], l2, of(rb, 3))
-        w2_g = keep.tile([P, H, PACK], BF16, name="w2_g", align_bytes=64)
-        nc.scalar.copy(*woven(w2_g, w2_raw, slice(0, H)))
+        w2_g = keep.tile([P, H, PACK], BF16, name="w2_g", tag="pa1", align_bytes=64)
+        nc.gpsimd.tensor_scalar(*woven(w2_g, w2_raw, slice(0, H)), 1.0, 0.0, ALU.mult, ALU.add)
         s_cast(z_pl, dt, 0)
         s_cast(z_pl, dt, 1)
         fetch2(2)

@@ -70,14 +70,15 @@ def tile_picked_tiepathborderduel_none_p_kernel(
 
         w1_g = keep.tile([P, PACK, P, PACK], BF16, name="w1_g", align_bytes=64)
         xs = keep.tile([P, S], U8, name="xs", align_bytes=64)
-        for h in range(2):
-            dst = w1_g[:, :, 64 * h : 64 * (h + 1), :].rearrange("p t m j -> p m j t")
-            src = w1_raw[h][:].rearrange("p j (m t) -> p m j t", t=PACK)
-            if h == 0:
-                nc.scalar.copy(dst, src)
-                nc.vector.tensor_copy(xs[:], xs_all[:].indirect(l_offs[:]))
-            else:
-                nc.vector.tensor_copy(dst, src)
+
+        def deal_w1(h, lo, hi):
+            return (w1_g[:, :, 64 * h + lo : 64 * h + hi, :].rearrange("p t m j -> p m j t"),
+                    w1_raw[h][:, :, PACK * lo : PACK * hi].rearrange("p j (m t) -> p m j t", t=PACK))
+
+        nc.scalar.copy(*deal_w1(0, 0, 64))
+        nc.vector.tensor_copy(xs[:], xs_all[:].indirect(l_offs[:]))
+        nc.vector.tensor_copy(*deal_w1(1, 0, 40))
+        nc.scalar.copy(*deal_w1(1, 40, 64))
         w1_c = keep.tile([P, H], U32, name="w1_c", align_bytes=64)
         w1_s = keep.tile([P, H], U8, name="w1_s", align_bytes=64)
         nc.vector.quantize_mx(out=w1_c[:].bitcast(FP8X4), scales=w1_s[:], in_=w1_g[:].rearrange("p t m j -> p (t m j)"))
@@ -123,8 +124,9 @@ def tile_picked_tiepathborderduel_none_p_kernel(
         y = f32_tiles("y", S)
         pa, pb, ra, rb = pair_tiles("pa"), pair_tiles("pb"), pair_tiles("ra"), pair_tiles("rb")
         dt = f32_tiles("dt", S)
-        pa2, pb2, diff, sa = pair_tiles("pa2"), pair_tiles("pb2"), pair_tiles("diff"), pair_tiles("sa")
-        z_pl = keep.tile([P, PACK, S], BF16, name="z_pl")
+        pa2, pb2, diff = pair_tiles("pa2"), pair_tiles("pb2"), pair_tiles("diff")
+        sa = [keep.tile([P, 2, W], F32, name="sa0"), None]
+        z_pl = shared.tile([P, PACK, S], BF16, name="z_pl", align_bytes=64, offset=8 * S)
 
         def s_gather(dst, window, lst):
             nc.scalar.activation(dst, window[:].indirect(lst), ACT.Copy)
@@ -183,30 +185,34 @@ def tile_picked_tiepathborderduel_none_p_kernel(
         put(dt[2], l2, of(rb, 2))
         put(dt[3], l2, of(rb, 3))
         w2_g = keep.tile([P, H, PACK], BF16, name="w2_g", tag="pa1", align_bytes=64)
-        nc.gpsimd.tensor_scalar(*woven(w2_g, w2_raw, slice(0, H)), 1.0, 0.0, ALU.mult, ALU.add)
+        nc.gpsimd.tensor_scalar(*woven(w2_g, w2_raw, half_cols[0]), 1.0, 0.0, ALU.mult, ALU.add)
         s_cast(z_pl, dt, 0)
         s_cast(z_pl, dt, 1)
         fetch2(2)
         fetch2(3)
+        nc.scalar.copy(*woven(w2_g, w2_raw, half_cols[1]))
         gate(sa, 0, 1.0)
         s_cast(z_pl, dt, 2)
-        sb = pair_tiles("sb")
-        gate(sb, 0, -1.0)
-        z_g = shared.tile([P, S, PACK], BF16, name="z_g", align_bytes=64, offset=0)
-        z_c, z_s = codes("z")
-        v1_cols, s1_cols = slice(0, 256), slice(256, S)
-        v_cast(z_pl, dt, 3)
+        sub2(1)
+        sb = [None, keep.tile([P, 2, W], F32, name="sb1")]
+        s_cast(z_pl, dt, 3)
         w2_c, w2_s = codes("w2")
         quantize(w2_c, w2_s, w2_g, slice(0, H))
+        z_g = shared.tile([P, S, PACK], BF16, name="z_g", align_bytes=64, offset=0)
+        z_c, z_s = codes("z")
+        v1_cols, s1_cols = slice(0, 192), slice(192, S)
+        dt2 = [keep.tile([P, S], F32, name="dt2_0")]
+        put_mul(dt2[0], l3, of(pa2, 0), of(sa, 0))
         nc.vector.tensor_copy(*woven(z_g, z_pl, v1_cols))
         nc.scalar.copy(*woven(z_g, z_pl, s1_cols))
-        sub2(1)
         quantize(z_c, z_s, z_g, slice(0, S))
-        dt2 = [shared.tile([P, S], F32, name=f"dt2_{t}", align_bytes=64, offset=4 * S * t) for t in range(2)]
-        dt2 += [keep.tile([P, S], F32, name=f"dt2_{t}") for t in (2, 3)]
+        dt2 += [shared.tile([P, S], F32, name=f"dt2_{t}", align_bytes=64, offset=4 * S * (t - 1)) for t in (1, 2)]
+        dt2 += [keep.tile([P, S], F32, name="dt2_3")]
+        sa[1] = shared.tile([P, 2, W], F32, name="sa1", align_bytes=64, offset=8 * S)
+        sb[0] = shared.tile([P, 2, W], F32, name="sb0", align_bytes=64, offset=12 * S)
+        gate(sb, 0, -1.0)
         gate(sa, 1, 1.0)
         gate(sb, 1, -1.0)
-        put_mul(dt2[0], l3, of(pa2, 0), of(sa, 0))
         put_mul(dt2[1], l3, of(pa2, 1), of(sa, 1))
         a_ps = [bank(i) for i in (6, 7, 0, 1)]
         for m in range(PACK):
@@ -242,23 +248,18 @@ def tile_picked_tiepathborderduel_none_p_kernel(
         z2_pl = keep.tile([P, PACK, S], BF16, name="z2_pl", tag="a_w1")
         s_cast(z2_pl, dt2, 0)
         s_cast(z2_pl, dt2, 1)
-        gather_a(2)
+        s_gather(a5[2][:], a_w[2], l5[:])
         s_cast(z2_pl, dt2, 2)
-        s_gather(a5[3][:], a_w[3], l5[:])
+        s_gather(a6[2][:], a_w[2], l6[:])
         z2_g = [keep.tile([P, HALF, PACK], BF16, name=f"z2_g{h}", align_bytes=64) for h in range(2)]
         z2_c, z2_s = codes("z2")
         for cols in half_cols:
             v_cast(z2_pl, dt2, 3, cols)
-        def weave(h, lo, hi):
-            return (z2_g[h][:, lo - h * HALF : hi - h * HALF, :].rearrange("p (c i) t -> p c t i", i=4),
-                    z2_pl[:, :, lo:hi].rearrange("p t (c i) -> p c t i", i=4))
-
-        nc.vector.tensor_copy(*weave(0, 0, HALF))
-        nc.scalar.copy(*weave(1, 384, S))
-        nc.vector.tensor_copy(*weave(1, HALF, 384))
+        for h, cols in enumerate(half_cols):
+            nc.vector.tensor_copy(z2_g[h][:].rearrange("p (c i) t -> p c t i", i=4), z2_pl[:, :, cols].rearrange("p t (c i) -> p c t i", i=4))
         for h, cols in enumerate(half_cols):
             nc.vector.quantize_mx(out=z2_c[:, cols].bitcast(FP8X4), scales=z2_s[:, cols], in_=z2_g[h][:].rearrange("p c t -> p (c t)"))
-        s_gather(a6[3][:], a_w[3], l6[:])
+        gather_a(3)
         b0_ps = [bank(2, HALF), bank(3, HALF)]
         b_ps = [None] + [bank(i) for i in (4, 5, 6)]
         for h in range(2):
@@ -266,21 +267,34 @@ def tile_picked_tiepathborderduel_none_p_kernel(
         for m in range(1, PACK):
             mm(b_ps[m][:], m, w2_c, w2_s, z2_c, z2_s, slice(0, S))
 
-        b7, b8, s1, s2, res = f32_tiles("b7", S), f32_tiles("b8", S), f32_tiles("s1", S), f32_tiles("s2", S), f32_tiles("res", S)
-        nc.scalar.copy(b_w[0][:, half_cols[0]], b0_ps[0][:])
+        b7 = keep.tile([P, S], F32, name="b7")
+        b8, s1, s2, res = f32_tiles("b8", S), f32_tiles("s1", S), f32_tiles("s2", S), f32_tiles("res", S)
+        nc.vector.tensor_copy(b_w[0][:, half_cols[0]], b0_ps[0][:])
         nc.vector.tensor_copy(b_w[0][:, half_cols[1]], b0_ps[1][:])
-        for m in range(PACK):
-            if m + 1 < PACK:
-                nc.scalar.copy(b_w[m + 1][:, :S], b_ps[m + 1][:])
-            whole = [(slice(0, S), l7[:], l8[:])]
-            parts = [(cols, part7, part8) for (cols, part7), (same, part8) in zip(halves(l7), halves(l8))]
-            for h, (cols, part7, part8) in enumerate(whole if m < PACK - 1 else parts):
-                s_gather(b8[m][:, cols], b_w[m], part8)
-                if m < 3 or (m == PACK - 1 and h < 1):
-                    nc.vector.tensor_tensor(s1[m][:, cols], b_w[m][:].indirect(part7), a5[m][:, cols], ALU.add)
-                else:
-                    s_gather(b7[m][:, cols], b_w[m], part7)
-                    nc.vector.tensor_tensor(s1[m][:, cols], b7[m][:, cols], a5[m][:, cols], ALU.add)
-                nc.vector.tensor_tensor(s2[m][:, cols], b8[m][:, cols], a6[m][:, cols], ALU.add)
-                nc.vector.tensor_tensor(res[m][:, cols], s1[m][:, cols], s2[m][:, cols], ALU.max)
-                nc.sync.dma_start(out[m * P : (m + 1) * P, cols], res[m][:, cols])
+
+        def finish(m, cols):
+            nc.vector.tensor_tensor(res[m][:, cols], s1[m][:, cols], s2[m][:, cols], ALU.max)
+            nc.sync.dma_start(out[m * P : (m + 1) * P, cols], res[m][:, cols])
+
+        last = PACK - 1
+        for m in range(last):
+            nc.scalar.copy(b_w[m + 1][:, :S], b_ps[m + 1][:])
+            nc.vector.tensor_tensor(s1[m][:], b_w[m][:].indirect(l7[:]), a5[m][:], ALU.add)
+            s_gather(b8[m][:], b_w[m], l8[:])
+            if m > 0:
+                nc.vector.tensor_tensor(s2[m - 1][:], b8[m - 1][:], a6[m - 1][:], ALU.add)
+                finish(m - 1, slice(0, S))
+        s_gather(b8[last][:], b_w[last], l8[:])
+        for h, (cols, part) in enumerate(halves(l7)):
+            if h >= 0:
+                s_gather(b7[:, cols], b_w[last], part)
+        nc.vector.tensor_tensor(s2[last - 1][:], b8[last - 1][:], a6[last - 1][:], ALU.add)
+        finish(last - 1, slice(0, S))
+        nc.vector.tensor_tensor(s2[last][:], b8[last][:], a6[last][:], ALU.add)
+        for h, (cols, part) in enumerate(halves(l7)):
+            if h >= 0:
+                nc.vector.tensor_tensor(s1[last][:, cols], b7[:, cols], a5[last][:, cols], ALU.add)
+            else:
+                nc.vector.tensor_tensor(s1[last][:, cols], b_w[last][:].indirect(part), a5[last][:, cols], ALU.add)
+        for cols in half_cols:
+            finish(last, cols)

@@ -2,8 +2,8 @@ from contextlib import ExitStack
 
 import concourse.mybir as mybir
 
-K, T, S, H, W = 512, 2048, 512, 512, 256
-FLOPS = 3 * 2 * 512 * 512 * 512
+T, S, H, W = 2048, 512, 512, 256
+FLOPS = 3 * 2 * H * H * S
 
 F32 = mybir.dt.float32
 BF16 = mybir.dt.bfloat16
@@ -18,7 +18,14 @@ ACT = mybir.ActivationFunctionType
 P = 128
 PACK = 4
 HALF = 256
+GROUP = 16
 SPARE = 16
+RUN = 4
+W1_VECTOR = 40
+Z_VECTOR = 192
+F32_TILE = 4 * S
+ALL = slice(0, S)
+HALVES = (slice(0, HALF), slice(HALF, S))
 
 
 def tile_picked_tiepathborderduel_none_p_kernel(
@@ -32,24 +39,69 @@ def tile_picked_tiepathborderduel_none_p_kernel(
         psum = ctx.enter_context(tc.psum_pool(name="psum", bufs=1))
 
         def load_list(name, src):
-            t = lists.tile(list(src.shape), U16, name=name)
-            nc.sync.dma_start(t[:], src)
-            return t
+            tile = lists.tile(list(src.shape), U16, name=name)
+            nc.sync.dma_start(tile[:], src)
+            return tile
+
+        def list_halves(lst):
+            per_half = HALF // GROUP
+            return [(cols, lst[:, per_half * h : per_half * (h + 1)]) for h, cols in enumerate(HALVES)]
 
         def f32_tiles(name, width):
             return [keep.tile([P, width], F32, name=f"{name}{t}") for t in range(PACK)]
 
+        def pair_tiles(name):
+            return [keep.tile([P, 2, W], F32, name=f"{name}{u}", align_bytes=64) for u in range(2)]
+
+        def one(pairs, t):
+            return pairs[t // 2][:, t % 2, :]
+
+        def both(pairs, u):
+            return pairs[u][:].rearrange("p a w -> p (a w)")
+
+        def mx_tiles(name):
+            words = keep.tile([P, S], U32, name=f"{name}_words", align_bytes=64)
+            scales = keep.tile([P, S], U8, name=f"{name}_scales", align_bytes=64)
+            return words, scales
+
+        def weave(woven, planes):
+            return (
+                woven.rearrange("p (c i) j -> p c j i", i=RUN),
+                planes.rearrange("p j (c i) -> p c j i", i=RUN),
+            )
+
+        def quantize(mx, cols, woven):
+            words, scales = mx
+            nc.vector.quantize_mx(
+                out=words[:, cols].bitcast(FP8X4), scales=scales[:, cols], in_=woven.rearrange("p c j -> p (c j)")
+            )
+
+        def bank(i, width=S):
+            return psum.tile([P, width], F32, name=f"bank{i}")
+
+        def product(acc, weights, t, moving, cols):
+            rows = slice(t * P, (t + 1) * P)
+            nc.tensor.matmul_mx(
+                out=acc,
+                lhsT=weights[0][:, rows].bitcast(FP8X4),
+                lhsT_scale=weights[1][:, rows],
+                rhs=moving[0][:, cols].bitcast(FP8X4),
+                rhs_scale=moving[1][:, cols],
+                start=True,
+                stop=True,
+            )
+
         w1_rows = w1.rearrange("(p j) c -> p j c", j=PACK)
         w1_raw = [keep.tile([P, PACK, HALF], F32, name=f"w1_raw{h}") for h in range(2)]
-        nc.sync.dma_start(w1_raw[0][:], w1_rows[:, :, :HALF])
+        nc.sync.dma_start(w1_raw[0][:], w1_rows[:, :, HALVES[0]])
         l_offs = load_list("l_offs", offs)
         xs_all = keep.tile([P, T], U8, name="xs_all")
         nc.gpsimd.memset(xs_all[:].bitcast(I32), 0)
         for q in range(4):
             nc.sync.dma_start(xs_all[32 * q : 32 * q + 4, :].bitcast(I32), x_scales[0, 4 * q : 4 * q + 4, :].bitcast(I32))
-        nc.sync.dma_start(w1_raw[1][:], w1_rows[:, :, HALF:])
+        nc.sync.dma_start(w1_raw[1][:], w1_rows[:, :, HALVES[1]])
         xw_all = keep.tile([P, T], I32, name="xw_all")
-        nc.sync.dma_start(xw_all[:], x_words[0].rearrange("p n t -> p (n t)").bitcast(I32))
+        nc.sync.dma_start(xw_all[:], x_words[0].rearrange("p n j -> p (n j)").bitcast(I32))
         l1 = load_list("l1", n1)
         l2 = load_list("l2", n2)
         l3 = load_list("l3", n3)
@@ -63,238 +115,205 @@ def tile_picked_tiepathborderduel_none_p_kernel(
         l7 = load_list("l7", n7)
         l8 = load_list("l8", n8)
 
-        def halves(lst):
-            return [(slice(h * HALF, (h + 1) * HALF), lst[:, 16 * h : 16 * (h + 1)]) for h in range(2)]
-
-        half_cols = [slice(0, HALF), slice(HALF, S)]
-
-        w1_g = keep.tile([P, PACK, P, PACK], BF16, name="w1_g", align_bytes=64)
+        w1_woven = keep.tile([P, PACK, P, PACK], BF16, name="w1_woven", align_bytes=64)
         xs = keep.tile([P, S], U8, name="xs", align_bytes=64)
+        groups = HALF // PACK
 
         def deal_w1(h, lo, hi):
-            return (w1_g[:, :, 64 * h + lo : 64 * h + hi, :].rearrange("p t m j -> p m j t"),
-                    w1_raw[h][:, :, PACK * lo : PACK * hi].rearrange("p j (m t) -> p m j t", t=PACK))
+            return (
+                w1_woven[:, :, groups * h + lo : groups * h + hi, :].rearrange("p t m j -> p m j t"),
+                w1_raw[h][:, :, PACK * lo : PACK * hi].rearrange("p j (m t) -> p m j t", t=PACK),
+            )
 
-        nc.scalar.copy(*deal_w1(0, 0, 64))
+        nc.scalar.copy(*deal_w1(0, 0, groups))
         nc.vector.tensor_copy(xs[:], xs_all[:].indirect(l_offs[:]))
-        nc.vector.tensor_copy(*deal_w1(1, 0, 40))
-        nc.scalar.copy(*deal_w1(1, 40, 64))
-        w1_c = keep.tile([P, H], U32, name="w1_c", align_bytes=64)
-        w1_s = keep.tile([P, H], U8, name="w1_s", align_bytes=64)
-        nc.vector.quantize_mx(out=w1_c[:].bitcast(FP8X4), scales=w1_s[:], in_=w1_g[:].rearrange("p t m j -> p (t m j)"))
+        nc.vector.tensor_copy(*deal_w1(1, 0, W1_VECTOR))
+        nc.scalar.copy(*deal_w1(1, W1_VECTOR, groups))
+        w1_mx = mx_tiles("w1")
+        quantize(w1_mx, ALL, w1_woven[:].rearrange("p t m j -> p (t m) j"))
 
         xw = keep.tile([P, S], U32, name="xw", align_bytes=64)
-        for cols, part in halves(l_offs):
-            nc.vector.tensor_copy(xw[:, cols], xw_all[:].bitcast(U32).indirect(part))
-
-        def mm(bank, t, w_c, w_s, r_c, r_s, cols):
-            rows = slice(t * P, (t + 1) * P)
-            nc.tensor.matmul_mx(out=bank, lhsT=w_c[:, rows].bitcast(FP8X4), lhsT_scale=w_s[:, rows],
-                                rhs=r_c[:, cols].bitcast(FP8X4), rhs_scale=r_s[:, cols], start=True, stop=True)
-
-        def bank(i, width=S):
-            return psum.tile([P, width], F32, name=f"bank{i}")
-
+        for cols, offsets in list_halves(l_offs):
+            nc.vector.tensor_copy(xw[:, cols], xw_all[:].bitcast(U32).indirect(offsets))
+        x_mx = (xw, xs)
         y_half_ps = [[bank(2 * t + h, HALF) for h in range(2)] for t in range(2)]
         y_ps = {t: bank(2 + t) for t in (2, 3)}
-        for h in range(2):
+        for h, cols in enumerate(HALVES):
             for t in range(2):
-                mm(y_half_ps[t][h][:], t, w1_c, w1_s, xw, xs, half_cols[h])
+                product(y_half_ps[t][h][:], w1_mx, t, x_mx, cols)
         for t in (2, 3):
-            mm(y_ps[t][:], t, w1_c, w1_s, xw, xs, slice(0, S))
-
-        def woven(dst, src, cols):
-            return (dst[:, cols, :].rearrange("p (c i) t -> p c t i", i=4), src[:, :, cols].rearrange("p t (c i) -> p c t i", i=4))
-
-        def codes(name):
-            return (keep.tile([P, S], U32, name=f"{name}_c", align_bytes=64), keep.tile([P, S], U8, name=f"{name}_s", align_bytes=64))
-
-        def quantize(c, s, grouped, cols):
-            nc.vector.quantize_mx(out=c[:, cols].bitcast(FP8X4), scales=s[:, cols], in_=grouped[:, cols, :].rearrange("p c t -> p (c t)"))
-
-        def pair_tiles(name):
-            return [keep.tile([P, 2, W], F32, name=f"{name}{u}", align_bytes=64) for u in range(2)]
-
-        def of(pairs, t):
-            return pairs[t // 2][:, t % 2, :]
-
-        def both(pairs, u):
-            return pairs[u][:].rearrange("p a w -> p (a w)")
+            product(y_ps[t][:], w1_mx, t, x_mx, ALL)
 
         y = f32_tiles("y", S)
         pa, pb, ra, rb = pair_tiles("pa"), pair_tiles("pb"), pair_tiles("ra"), pair_tiles("rb")
         dt = f32_tiles("dt", S)
-        pa2, pb2, diff = pair_tiles("pa2"), pair_tiles("pb2"), pair_tiles("diff")
-        sa = [keep.tile([P, 2, W], F32, name="sa0"), None]
-        z_pl = shared.tile([P, PACK, S], BF16, name="z_pl", align_bytes=64, offset=8 * S)
+        pa2, pb2 = pair_tiles("pa2_"), pair_tiles("pb2_")
+        gate_a = [keep.tile([P, 2, W], F32, name="gate_a0")]
+        z_planes = shared.tile([P, PACK, S], BF16, name="z_planes", align_bytes=64, offset=2 * F32_TILE)
 
-        def s_gather(dst, window, lst):
-            nc.scalar.activation(dst, window[:].indirect(lst), ACT.Copy)
+        def gather(dst, window, offsets):
+            nc.scalar.activation(dst, window[:].indirect(offsets), ACT.Copy)
 
-        def fetch1(t):
-            s_gather(of(pa, t), y[t], l1[:])
-            s_gather(of(pb, t), y[t], l2[:])
+        def fetch_first(t):
+            gather(one(pa, t), y[t], l1[:])
+            gather(one(pb, t), y[t], l2[:])
+
+        def fetch_second(t):
+            gather(one(pa2, t), y[t], l3[:])
+            gather(one(pb2, t), y[t], l4[:])
 
         def put(window, lst, values):
             nc.vector.tensor_copy(window[:].indirect(lst[:]), values)
 
-        def put_mul(window, lst, values, factor):
-            nc.vector.tensor_tensor(window[:].indirect(lst[:]), values, factor, ALU.mult)
+        def put_gated(window, lst, values, gates):
+            nc.vector.tensor_tensor(window[:].indirect(lst[:]), values, gates, ALU.mult)
 
-        def fetch2(t):
-            s_gather(of(pa2, t), y[t], l3[:])
-            s_gather(of(pb2, t), y[t], l4[:])
-
-        def sub2(u):
+        def subtract(u):
             nc.gpsimd.tensor_tensor(both(diff, u), both(pa2, u), both(pb2, u), ALU.subtract)
 
-        def gate(dst, u, sign):
-            nc.scalar.activation(both(dst, u), both(diff, u), ACT.Sigmoid, scale=sign)
+        def sigmoid(gates, u, sign):
+            nc.scalar.activation(gates[:].rearrange("p a w -> p (a w)"), both(diff, u), ACT.Sigmoid, scale=sign)
 
-        def s_cast(planes, src, t, cols=slice(0, S)):
-            nc.scalar.activation(planes[:, t, cols], src[t][:, cols], ACT.Copy, scale=gain[:, t : t + 1])
+        def scale_round(planes, src, t):
+            nc.scalar.activation(planes[:, t, ALL], src[t][:, ALL], ACT.Copy, scale=gain[:, t : t + 1])
 
-        def v_cast(planes, src, t, cols=slice(0, S)):
-            nc.vector.tensor_scalar(planes[:, t, cols], src[t][:, cols], gain[:, t : t + 1], None, ALU.mult)
-
-        nc.scalar.copy(y[0][:, half_cols[0]], y_half_ps[0][0][:])
-        nc.scalar.copy(y[1][:, half_cols[0]], y_half_ps[1][0][:])
-        nc.vector.tensor_copy(y[0][:, half_cols[1]], y_half_ps[0][1][:])
-        nc.scalar.copy(y[1][:, half_cols[1]], y_half_ps[1][1][:])
-        s_gather(of(pa, 0), y[0], l1[:])
-        nc.vector.tensor_copy(of(pb, 0), y[0][:].indirect(l2[:]))
-        nc.vector.tensor_tensor(of(ra, 0), of(pa, 0), of(pb, 0), ALU.max)
-        put(dt[0], l1, of(ra, 0))
-        fetch1(1)
-        nc.vector.tensor_tensor(of(ra, 1), of(pa, 1), of(pb, 1), ALU.max)
+        nc.scalar.copy(y[0][:, HALVES[0]], y_half_ps[0][0][:])
+        nc.scalar.copy(y[1][:, HALVES[0]], y_half_ps[1][0][:])
+        nc.vector.tensor_copy(y[0][:, HALVES[1]], y_half_ps[0][1][:])
+        nc.scalar.copy(y[1][:, HALVES[1]], y_half_ps[1][1][:])
+        gather(one(pa, 0), y[0], l1[:])
+        nc.vector.tensor_copy(one(pb, 0), y[0][:].indirect(l2[:]))
+        nc.vector.tensor_tensor(one(ra, 0), one(pa, 0), one(pb, 0), ALU.max)
+        put(dt[0], l1, one(ra, 0))
+        fetch_first(1)
+        nc.vector.tensor_tensor(one(ra, 1), one(pa, 1), one(pb, 1), ALU.max)
         nc.vector.tensor_tensor(both(rb, 0), both(pa, 0), both(pb, 0), ALU.min)
-        put(dt[1], l1, of(ra, 1))
-        put(dt[0], l2, of(rb, 0))
-        put(dt[1], l2, of(rb, 1))
+        put(dt[1], l1, one(ra, 1))
+        for t in (0, 1):
+            put(dt[t], l2, one(rb, t))
         for t in (2, 3):
             nc.scalar.copy(y[t][:], y_ps[t][:])
-        fetch2(0)
-        fetch2(1)
-        sub2(0)
-        fetch1(2)
-        fetch1(3)
+        for t in (2, 3):
+            fetch_first(t)
         nc.vector.tensor_tensor(both(ra, 1), both(pa, 1), both(pb, 1), ALU.max)
         nc.vector.tensor_tensor(both(rb, 1), both(pa, 1), both(pb, 1), ALU.min)
-        put(dt[2], l1, of(ra, 2))
-        put(dt[3], l1, of(ra, 3))
-        put(dt[2], l2, of(rb, 2))
-        put(dt[3], l2, of(rb, 3))
-        w2_g = keep.tile([P, H, PACK], BF16, name="w2_g", tag="pa1", align_bytes=64)
-        nc.gpsimd.tensor_scalar(*woven(w2_g, w2_raw, half_cols[0]), 1.0, 0.0, ALU.mult, ALU.add)
-        s_cast(z_pl, dt, 0)
-        s_cast(z_pl, dt, 1)
-        fetch2(2)
-        fetch2(3)
-        nc.scalar.copy(*woven(w2_g, w2_raw, half_cols[1]))
-        gate(sa, 0, 1.0)
-        s_cast(z_pl, dt, 2)
-        sub2(1)
-        sb = [None, keep.tile([P, 2, W], F32, name="sb1")]
-        s_cast(z_pl, dt, 3)
-        w2_c, w2_s = codes("w2")
-        quantize(w2_c, w2_s, w2_g, slice(0, H))
-        z_g = shared.tile([P, S, PACK], BF16, name="z_g", align_bytes=64, offset=0)
-        z_c, z_s = codes("z")
-        v1_cols, s1_cols = slice(0, 192), slice(192, S)
+        for t in (2, 3):
+            put(dt[t], l1, one(ra, t))
+        for t in (2, 3):
+            put(dt[t], l2, one(rb, t))
+
+        diff = [keep.tile([P, 2, W], F32, name="diff0", tag="pb1", align_bytes=64), keep.tile([P, 2, W], F32, name="diff1")]
+        for t in (0, 1):
+            fetch_second(t)
+        subtract(0)
+        w2_woven = keep.tile([P, H, PACK], BF16, name="w2_woven", tag="pa0", align_bytes=64)
+        nc.gpsimd.tensor_scalar(*weave(w2_woven[:, HALVES[0], :], w2_raw[:, :, HALVES[0]]), 1.0, 0.0, ALU.mult, ALU.add)
+        for t in (0, 1):
+            scale_round(z_planes, dt, t)
+        for t in (2, 3):
+            fetch_second(t)
+        nc.scalar.copy(*weave(w2_woven[:, HALVES[1], :], w2_raw[:, :, HALVES[1]]))
+        sigmoid(gate_a[0], 0, 1.0)
+        scale_round(z_planes, dt, 2)
+        subtract(1)
+        gate_b1 = keep.tile([P, 2, W], F32, name="gate_b1")
+        scale_round(z_planes, dt, 3)
+        w2_mx = mx_tiles("w2")
+        quantize(w2_mx, ALL, w2_woven[:])
+
+        z_woven = shared.tile([P, S, PACK], BF16, name="z_woven", align_bytes=64, offset=0)
+        z_mx = mx_tiles("z")
         dt2 = [keep.tile([P, S], F32, name="dt2_0")]
-        put_mul(dt2[0], l3, of(pa2, 0), of(sa, 0))
-        nc.vector.tensor_copy(*woven(z_g, z_pl, v1_cols))
-        nc.scalar.copy(*woven(z_g, z_pl, s1_cols))
-        quantize(z_c, z_s, z_g, slice(0, S))
-        dt2 += [shared.tile([P, S], F32, name=f"dt2_{t}", align_bytes=64, offset=4 * S * (t - 1)) for t in (1, 2)]
+        put_gated(dt2[0], l3, one(pa2, 0), one(gate_a, 0))
+        nc.vector.tensor_copy(*weave(z_woven[:, :Z_VECTOR, :], z_planes[:, :, :Z_VECTOR]))
+        nc.scalar.copy(*weave(z_woven[:, Z_VECTOR:, :], z_planes[:, :, Z_VECTOR:]))
+        quantize(z_mx, ALL, z_woven[:])
+
+        dt2 += [shared.tile([P, S], F32, name=f"dt2_{t}", align_bytes=64, offset=(t - 1) * F32_TILE) for t in (1, 2)]
         dt2 += [keep.tile([P, S], F32, name="dt2_3")]
-        sa[1] = shared.tile([P, 2, W], F32, name="sa1", align_bytes=64, offset=8 * S)
-        sb[0] = shared.tile([P, 2, W], F32, name="sb0", align_bytes=64, offset=12 * S)
-        gate(sb, 0, -1.0)
-        gate(sa, 1, 1.0)
-        gate(sb, 1, -1.0)
-        put_mul(dt2[1], l3, of(pa2, 1), of(sa, 1))
+        gate_a += [shared.tile([P, 2, W], F32, name="gate_a1", align_bytes=64, offset=2 * F32_TILE)]
+        gate_b = [shared.tile([P, 2, W], F32, name="gate_b0", align_bytes=64, offset=3 * F32_TILE), gate_b1]
+        sigmoid(gate_b[0], 0, -1.0)
+        sigmoid(gate_a[1], 1, 1.0)
+        sigmoid(gate_b[1], 1, -1.0)
+        put_gated(dt2[1], l3, one(pa2, 1), one(gate_a, 1))
         a_ps = [bank(i) for i in (6, 7, 0, 1)]
         for m in range(PACK):
-            mm(a_ps[m][:], m, w2_c, w2_s, z_c, z_s, slice(0, S))
+            product(a_ps[m][:], w2_mx, m, z_mx, ALL)
 
         def windows(name):
             tiles = f32_tiles(name, S + SPARE)
-            for t in tiles:
-                nc.gpsimd.memset(t[:, S:], 0.0)
+            for tile in tiles:
+                nc.gpsimd.memset(tile[:, S:], 0.0)
             return tiles
 
-        a_w, b_w = windows("a_w"), windows("b_w")
-        a5, a6 = f32_tiles("a5", S), f32_tiles("a6", S)
+        a, b = windows("a"), windows("b")
+        a5, a6 = f32_tiles("a5_", S), f32_tiles("a6_", S)
+        for t in (0, 1):
+            put_gated(dt2[t], l4, one(pb2, t), one(gate_b, t))
+        for t in (2, 3):
+            put_gated(dt2[t], l3, one(pa2, t), one(gate_a, t))
+        for t in (2, 3):
+            put_gated(dt2[t], l4, one(pb2, t), one(gate_b, t))
 
-        def gather_a(m):
-            s_gather(a5[m][:], a_w[m], l5[:])
-            s_gather(a6[m][:], a_w[m], l6[:])
-
-        put_mul(dt2[0], l4, of(pb2, 0), of(sb, 0))
-        put_mul(dt2[1], l4, of(pb2, 1), of(sb, 1))
-        put_mul(dt2[2], l3, of(pa2, 2), of(sa, 2))
-        put_mul(dt2[3], l3, of(pa2, 3), of(sa, 3))
-        put_mul(dt2[2], l4, of(pb2, 2), of(sb, 2))
-        put_mul(dt2[3], l4, of(pb2, 3), of(sb, 3))
-
-        def evac_a(m):
-            nc.scalar.copy(a_w[m][:, :S], a_ps[m][:])
+        def fetch_a(m):
+            gather(a5[m][:], a[m], l5[:])
+            gather(a6[m][:], a[m], l6[:])
 
         for m in range(PACK):
-            evac_a(m)
-        gather_a(0)
-        gather_a(1)
-        z2_pl = keep.tile([P, PACK, S], BF16, name="z2_pl", tag="a_w1")
-        s_cast(z2_pl, dt2, 0)
-        s_cast(z2_pl, dt2, 1)
-        s_gather(a5[2][:], a_w[2], l5[:])
-        s_cast(z2_pl, dt2, 2)
-        s_gather(a6[2][:], a_w[2], l6[:])
-        z2_g = [keep.tile([P, HALF, PACK], BF16, name=f"z2_g{h}", align_bytes=64) for h in range(2)]
-        z2_c, z2_s = codes("z2")
-        for cols in half_cols:
-            v_cast(z2_pl, dt2, 3, cols)
-        for h, cols in enumerate(half_cols):
-            nc.vector.tensor_copy(z2_g[h][:].rearrange("p (c i) t -> p c t i", i=4), z2_pl[:, :, cols].rearrange("p t (c i) -> p c t i", i=4))
-        for h, cols in enumerate(half_cols):
-            nc.vector.quantize_mx(out=z2_c[:, cols].bitcast(FP8X4), scales=z2_s[:, cols], in_=z2_g[h][:].rearrange("p c t -> p (c t)"))
-        gather_a(3)
-        b0_ps = [bank(2, HALF), bank(3, HALF)]
-        b_ps = [None] + [bank(i) for i in (4, 5, 6)]
-        for h in range(2):
-            mm(b0_ps[h][:], 0, w2_c, w2_s, z2_c, z2_s, half_cols[h])
-        for m in range(1, PACK):
-            mm(b_ps[m][:], m, w2_c, w2_s, z2_c, z2_s, slice(0, S))
-
-        b7 = keep.tile([P, S], F32, name="b7")
-        b8, s1, s2, res = f32_tiles("b8", S), f32_tiles("s1", S), f32_tiles("s2", S), f32_tiles("res", S)
-        nc.vector.tensor_copy(b_w[0][:, half_cols[0]], b0_ps[0][:])
-        nc.vector.tensor_copy(b_w[0][:, half_cols[1]], b0_ps[1][:])
-
-        def finish(m, cols):
-            nc.vector.tensor_tensor(res[m][:, cols], s1[m][:, cols], s2[m][:, cols], ALU.max)
-            nc.sync.dma_start(out[m * P : (m + 1) * P, cols], res[m][:, cols])
+            nc.scalar.copy(a[m][:, :S], a_ps[m][:])
+        for m in (0, 1):
+            fetch_a(m)
+        z2_planes = keep.tile([P, PACK, S], BF16, name="z2_planes", tag="a1")
+        for t in (0, 1):
+            scale_round(z2_planes, dt2, t)
+        gather(a5[2][:], a[2], l5[:])
+        scale_round(z2_planes, dt2, 2)
+        gather(a6[2][:], a[2], l6[:])
 
         last = PACK - 1
+        z2_woven = [keep.tile([P, HALF, PACK], BF16, name=f"z2_woven{h}", align_bytes=64) for h in range(2)]
+        z2_mx = mx_tiles("z2")
+        for cols in HALVES:
+            nc.vector.tensor_scalar(z2_planes[:, last, cols], dt2[last][:, cols], gain[:, last : last + 1], None, ALU.mult)
+        for h, cols in enumerate(HALVES):
+            nc.vector.tensor_copy(*weave(z2_woven[h][:], z2_planes[:, :, cols]))
+        for h, cols in enumerate(HALVES):
+            quantize(z2_mx, cols, z2_woven[h][:])
+        fetch_a(last)
+        b0_ps = [bank(2, HALF), bank(3, HALF)]
+        b_ps = {m: bank(3 + m) for m in range(1, PACK)}
+        for h, cols in enumerate(HALVES):
+            product(b0_ps[h][:], w2_mx, 0, z2_mx, cols)
+        for m in range(1, PACK):
+            product(b_ps[m][:], w2_mx, m, z2_mx, ALL)
+
+        b7_last = keep.tile([P, S], F32, name="b7_last")
+        b8, sum7, sum8, res = f32_tiles("b8_", S), f32_tiles("sum7_", S), f32_tiles("sum8_", S), f32_tiles("res", S)
+        for h, cols in enumerate(HALVES):
+            nc.vector.tensor_copy(b[0][:, cols], b0_ps[h][:])
+
+        def add8(m):
+            nc.vector.tensor_tensor(sum8[m][:], b8[m][:], a6[m][:], ALU.add)
+
+        def finish(m, cols):
+            nc.vector.tensor_tensor(res[m][:, cols], sum7[m][:, cols], sum8[m][:, cols], ALU.max)
+            nc.sync.dma_start(out[m * P : (m + 1) * P, cols], res[m][:, cols])
+
         for m in range(last):
-            nc.scalar.copy(b_w[m + 1][:, :S], b_ps[m + 1][:])
-            nc.vector.tensor_tensor(s1[m][:], b_w[m][:].indirect(l7[:]), a5[m][:], ALU.add)
-            s_gather(b8[m][:], b_w[m], l8[:])
+            nc.scalar.copy(b[m + 1][:, :S], b_ps[m + 1][:])
+            nc.vector.tensor_tensor(sum7[m][:], b[m][:].indirect(l7[:]), a5[m][:], ALU.add)
+            gather(b8[m][:], b[m], l8[:])
             if m > 0:
-                nc.vector.tensor_tensor(s2[m - 1][:], b8[m - 1][:], a6[m - 1][:], ALU.add)
-                finish(m - 1, slice(0, S))
-        s_gather(b8[last][:], b_w[last], l8[:])
-        for h, (cols, part) in enumerate(halves(l7)):
-            if h >= 0:
-                s_gather(b7[:, cols], b_w[last], part)
-        nc.vector.tensor_tensor(s2[last - 1][:], b8[last - 1][:], a6[last - 1][:], ALU.add)
-        finish(last - 1, slice(0, S))
-        nc.vector.tensor_tensor(s2[last][:], b8[last][:], a6[last][:], ALU.add)
-        for h, (cols, part) in enumerate(halves(l7)):
-            if h >= 0:
-                nc.vector.tensor_tensor(s1[last][:, cols], b7[:, cols], a5[last][:, cols], ALU.add)
-            else:
-                nc.vector.tensor_tensor(s1[last][:, cols], b_w[last][:].indirect(part), a5[last][:, cols], ALU.add)
-        for cols in half_cols:
+                add8(m - 1)
+                finish(m - 1, ALL)
+        gather(b8[last][:], b[last], l8[:])
+        for cols, offsets in list_halves(l7):
+            gather(b7_last[:, cols], b[last], offsets)
+        add8(last - 1)
+        finish(last - 1, ALL)
+        add8(last)
+        for cols in HALVES:
+            nc.vector.tensor_tensor(sum7[last][:, cols], b7_last[:, cols], a5[last][:, cols], ALU.add)
+        for cols in HALVES:
             finish(last, cols)

from contextlib import ExitStack

import concourse.mybir as mybir

T, S, H, W = 2048, 512, 512, 256
FLOPS = 3 * 2 * H * H * S

F32 = mybir.dt.float32
BF16 = mybir.dt.bfloat16
I32 = mybir.dt.int32
U32 = mybir.dt.uint32
U16 = mybir.dt.uint16
U8 = mybir.dt.uint8
FP8X4 = mybir.dt.float8_e4m3fn_x4
ALU = mybir.AluOpType
ACT = mybir.ActivationFunctionType

P = 128
PACK = 4
HALF = 256
GROUP = 16
SPARE = 16
RUN = 4
W1_VECTOR = 40
Z_VECTOR = 192
F32_TILE = 4 * S
ALL = slice(0, S)
HALVES = (slice(0, HALF), slice(HALF, S))


def tile_picked_tiepathborderduel_none_p_kernel(
    tc, x_words, x_scales, w1, gn, w2, offs, n1, n2, n3, n4, n5, n6, n7, n8, out
):
    nc = tc.nc
    with ExitStack() as ctx:
        lists = ctx.enter_context(tc.tile_pool(name="lists", bufs=1))
        keep = ctx.enter_context(tc.tile_pool(name="keep", bufs=1))
        shared = ctx.enter_context(tc.tile_pool(name="shared", bufs=1))
        psum = ctx.enter_context(tc.psum_pool(name="psum", bufs=1))

        def load_list(name, src):
            tile = lists.tile(list(src.shape), U16, name=name)
            nc.sync.dma_start(tile[:], src)
            return tile

        def list_halves(lst):
            per_half = HALF // GROUP
            return [(cols, lst[:, per_half * h : per_half * (h + 1)]) for h, cols in enumerate(HALVES)]

        def f32_tiles(name, width):
            return [keep.tile([P, width], F32, name=f"{name}{t}") for t in range(PACK)]

        def pair_tiles(name):
            return [keep.tile([P, 2, W], F32, name=f"{name}{u}", align_bytes=64) for u in range(2)]

        def one(pairs, t):
            return pairs[t // 2][:, t % 2, :]

        def both(pairs, u):
            return pairs[u][:].rearrange("p a w -> p (a w)")

        def mx_tiles(name):
            words = keep.tile([P, S], U32, name=f"{name}_words", align_bytes=64)
            scales = keep.tile([P, S], U8, name=f"{name}_scales", align_bytes=64)
            return words, scales

        def weave(woven, planes):
            return (
                woven.rearrange("p (c i) j -> p c j i", i=RUN),
                planes.rearrange("p j (c i) -> p c j i", i=RUN),
            )

        def quantize(mx, cols, woven):
            words, scales = mx
            nc.vector.quantize_mx(
                out=words[:, cols].bitcast(FP8X4), scales=scales[:, cols], in_=woven.rearrange("p c j -> p (c j)")
            )

        def bank(i, width=S):
            return psum.tile([P, width], F32, name=f"bank{i}")

        def product(acc, weights, t, moving, cols):
            rows = slice(t * P, (t + 1) * P)
            nc.tensor.matmul_mx(
                out=acc,
                lhsT=weights[0][:, rows].bitcast(FP8X4),
                lhsT_scale=weights[1][:, rows],
                rhs=moving[0][:, cols].bitcast(FP8X4),
                rhs_scale=moving[1][:, cols],
                start=True,
                stop=True,
            )

        w1_rows = w1.rearrange("(p j) c -> p j c", j=PACK)
        w1_raw = [keep.tile([P, PACK, HALF], F32, name=f"w1_raw{h}") for h in range(2)]
        nc.sync.dma_start(w1_raw[0][:], w1_rows[:, :, HALVES[0]])
        l_offs = load_list("l_offs", offs)
        xs_all = keep.tile([P, T], U8, name="xs_all")
        nc.gpsimd.memset(xs_all[:].bitcast(I32), 0)
        for q in range(4):
            nc.sync.dma_start(xs_all[32 * q : 32 * q + 4, :].bitcast(I32), x_scales[0, 4 * q : 4 * q + 4, :].bitcast(I32))
        nc.sync.dma_start(w1_raw[1][:], w1_rows[:, :, HALVES[1]])
        xw_all = keep.tile([P, T], I32, name="xw_all")
        nc.sync.dma_start(xw_all[:], x_words[0].rearrange("p n j -> p (n j)").bitcast(I32))
        l1 = load_list("l1", n1)
        l2 = load_list("l2", n2)
        l3 = load_list("l3", n3)
        l4 = load_list("l4", n4)
        w2_raw = keep.tile([P, PACK, H], F32, name="w2_raw")
        nc.sync.dma_start(w2_raw[:], w2.rearrange("(p j) c -> p j c", j=PACK))
        gain = keep.tile([P, PACK], F32, name="gain")
        nc.sync.dma_start(gain[:], gn.rearrange("(p t) o -> p (t o)", t=PACK))
        l5 = load_list("l5", n5)
        l6 = load_list("l6", n6)
        l7 = load_list("l7", n7)
        l8 = load_list("l8", n8)

        w1_woven = keep.tile([P, PACK, P, PACK], BF16, name="w1_woven", align_bytes=64)
        xs = keep.tile([P, S], U8, name="xs", align_bytes=64)
        groups = HALF // PACK

        def deal_w1(h, lo, hi):
            return (
                w1_woven[:, :, groups * h + lo : groups * h + hi, :].rearrange("p t m j -> p m j t"),
                w1_raw[h][:, :, PACK * lo : PACK * hi].rearrange("p j (m t) -> p m j t", t=PACK),
            )

        nc.scalar.copy(*deal_w1(0, 0, groups))
        nc.vector.tensor_copy(xs[:], xs_all[:].indirect(l_offs[:]))
        nc.vector.tensor_copy(*deal_w1(1, 0, W1_VECTOR))
        nc.scalar.copy(*deal_w1(1, W1_VECTOR, groups))
        w1_mx = mx_tiles("w1")
        quantize(w1_mx, ALL, w1_woven[:].rearrange("p t m j -> p (t m) j"))

        xw = keep.tile([P, S], U32, name="xw", align_bytes=64)
        for cols, offsets in list_halves(l_offs):
            nc.vector.tensor_copy(xw[:, cols], xw_all[:].bitcast(U32).indirect(offsets))
        x_mx = (xw, xs)
        y_half_ps = [[bank(2 * t + h, HALF) for h in range(2)] for t in range(2)]
        y_ps = {t: bank(2 + t) for t in (2, 3)}
        for h, cols in enumerate(HALVES):
            for t in range(2):
                product(y_half_ps[t][h][:], w1_mx, t, x_mx, cols)
        for t in (2, 3):
            product(y_ps[t][:], w1_mx, t, x_mx, ALL)

        y = f32_tiles("y", S)
        pa, pb, ra, rb = pair_tiles("pa"), pair_tiles("pb"), pair_tiles("ra"), pair_tiles("rb")
        dt = f32_tiles("dt", S)
        pa2, pb2 = pair_tiles("pa2_"), pair_tiles("pb2_")
        gate_a = [keep.tile([P, 2, W], F32, name="gate_a0")]
        z_planes = shared.tile([P, PACK, S], BF16, name="z_planes", align_bytes=64, offset=2 * F32_TILE)

        def gather(dst, window, offsets):
            nc.scalar.activation(dst, window[:].indirect(offsets), ACT.Copy)

        def fetch_first(t):
            gather(one(pa, t), y[t], l1[:])
            gather(one(pb, t), y[t], l2[:])

        def fetch_second(t):
            gather(one(pa2, t), y[t], l3[:])
            gather(one(pb2, t), y[t], l4[:])

        def put(window, lst, values):
            nc.vector.tensor_copy(window[:].indirect(lst[:]), values)

        def put_gated(window, lst, values, gates):
            nc.vector.tensor_tensor(window[:].indirect(lst[:]), values, gates, ALU.mult)

        def subtract(u):
            nc.gpsimd.tensor_tensor(both(diff, u), both(pa2, u), both(pb2, u), ALU.subtract)

        def sigmoid(gates, u, sign):
            nc.scalar.activation(gates[:].rearrange("p a w -> p (a w)"), both(diff, u), ACT.Sigmoid, scale=sign)

        def scale_round(planes, src, t):
            nc.scalar.activation(planes[:, t, ALL], src[t][:, ALL], ACT.Copy, scale=gain[:, t : t + 1])

        nc.scalar.copy(y[0][:, HALVES[0]], y_half_ps[0][0][:])
        nc.scalar.copy(y[1][:, HALVES[0]], y_half_ps[1][0][:])
        nc.vector.tensor_copy(y[0][:, HALVES[1]], y_half_ps[0][1][:])
        nc.scalar.copy(y[1][:, HALVES[1]], y_half_ps[1][1][:])
        gather(one(pa, 0), y[0], l1[:])
        nc.vector.tensor_copy(one(pb, 0), y[0][:].indirect(l2[:]))
        nc.vector.tensor_tensor(one(ra, 0), one(pa, 0), one(pb, 0), ALU.max)
        put(dt[0], l1, one(ra, 0))
        fetch_first(1)
        nc.vector.tensor_tensor(one(ra, 1), one(pa, 1), one(pb, 1), ALU.max)
        nc.vector.tensor_tensor(both(rb, 0), both(pa, 0), both(pb, 0), ALU.min)
        put(dt[1], l1, one(ra, 1))
        for t in (0, 1):
            put(dt[t], l2, one(rb, t))
        for t in (2, 3):
            nc.scalar.copy(y[t][:], y_ps[t][:])
        for t in (2, 3):
            fetch_first(t)
        nc.vector.tensor_tensor(both(ra, 1), both(pa, 1), both(pb, 1), ALU.max)
        nc.vector.tensor_tensor(both(rb, 1), both(pa, 1), both(pb, 1), ALU.min)
        for t in (2, 3):
            put(dt[t], l1, one(ra, t))
        for t in (2, 3):
            put(dt[t], l2, one(rb, t))

        diff = [keep.tile([P, 2, W], F32, name="diff0", tag="pb1", align_bytes=64), keep.tile([P, 2, W], F32, name="diff1")]
        for t in (0, 1):
            fetch_second(t)
        subtract(0)
        w2_woven = keep.tile([P, H, PACK], BF16, name="w2_woven", tag="pa0", align_bytes=64)
        nc.gpsimd.tensor_scalar(*weave(w2_woven[:, HALVES[0], :], w2_raw[:, :, HALVES[0]]), 1.0, 0.0, ALU.mult, ALU.add)
        for t in (0, 1):
            scale_round(z_planes, dt, t)
        for t in (2, 3):
            fetch_second(t)
        nc.scalar.copy(*weave(w2_woven[:, HALVES[1], :], w2_raw[:, :, HALVES[1]]))
        sigmoid(gate_a[0], 0, 1.0)
        scale_round(z_planes, dt, 2)
        subtract(1)
        gate_b1 = keep.tile([P, 2, W], F32, name="gate_b1")
        scale_round(z_planes, dt, 3)
        w2_mx = mx_tiles("w2")
        quantize(w2_mx, ALL, w2_woven[:])

        z_woven = shared.tile([P, S, PACK], BF16, name="z_woven", align_bytes=64, offset=0)
        z_mx = mx_tiles("z")
        dt2 = [keep.tile([P, S], F32, name="dt2_0")]
        put_gated(dt2[0], l3, one(pa2, 0), one(gate_a, 0))
        nc.vector.tensor_copy(*weave(z_woven[:, :Z_VECTOR, :], z_planes[:, :, :Z_VECTOR]))
        nc.scalar.copy(*weave(z_woven[:, Z_VECTOR:, :], z_planes[:, :, Z_VECTOR:]))
        quantize(z_mx, ALL, z_woven[:])

        dt2 += [shared.tile([P, S], F32, name=f"dt2_{t}", align_bytes=64, offset=(t - 1) * F32_TILE) for t in (1, 2)]
        dt2 += [keep.tile([P, S], F32, name="dt2_3")]
        gate_a += [shared.tile([P, 2, W], F32, name="gate_a1", align_bytes=64, offset=2 * F32_TILE)]
        gate_b = [shared.tile([P, 2, W], F32, name="gate_b0", align_bytes=64, offset=3 * F32_TILE), gate_b1]
        sigmoid(gate_b[0], 0, -1.0)
        sigmoid(gate_a[1], 1, 1.0)
        sigmoid(gate_b[1], 1, -1.0)
        put_gated(dt2[1], l3, one(pa2, 1), one(gate_a, 1))
        a_ps = [bank(i) for i in (6, 7, 0, 1)]
        for m in range(PACK):
            product(a_ps[m][:], w2_mx, m, z_mx, ALL)

        def windows(name):
            tiles = f32_tiles(name, S + SPARE)
            for tile in tiles:
                nc.gpsimd.memset(tile[:, S:], 0.0)
            return tiles

        a, b = windows("a"), windows("b")
        a5, a6 = f32_tiles("a5_", S), f32_tiles("a6_", S)
        for t in (0, 1):
            put_gated(dt2[t], l4, one(pb2, t), one(gate_b, t))
        for t in (2, 3):
            put_gated(dt2[t], l3, one(pa2, t), one(gate_a, t))
        for t in (2, 3):
            put_gated(dt2[t], l4, one(pb2, t), one(gate_b, t))

        def fetch_a(m):
            gather(a5[m][:], a[m], l5[:])
            gather(a6[m][:], a[m], l6[:])

        for m in range(PACK):
            nc.scalar.copy(a[m][:, :S], a_ps[m][:])
        for m in (0, 1):
            fetch_a(m)
        z2_planes = keep.tile([P, PACK, S], BF16, name="z2_planes", tag="a1")
        for t in (0, 1):
            scale_round(z2_planes, dt2, t)
        gather(a5[2][:], a[2], l5[:])
        scale_round(z2_planes, dt2, 2)
        gather(a6[2][:], a[2], l6[:])

        last = PACK - 1
        z2_woven = [keep.tile([P, HALF, PACK], BF16, name=f"z2_woven{h}", align_bytes=64) for h in range(2)]
        z2_mx = mx_tiles("z2")
        for cols in HALVES:
            nc.vector.tensor_scalar(z2_planes[:, last, cols], dt2[last][:, cols], gain[:, last : last + 1], None, ALU.mult)
        for h, cols in enumerate(HALVES):
            nc.vector.tensor_copy(*weave(z2_woven[h][:], z2_planes[:, :, cols]))
        for h, cols in enumerate(HALVES):
            quantize(z2_mx, cols, z2_woven[h][:])
        fetch_a(last)
        b0_ps = [bank(2, HALF), bank(3, HALF)]
        b_ps = {m: bank(3 + m) for m in range(1, PACK)}
        for h, cols in enumerate(HALVES):
            product(b0_ps[h][:], w2_mx, 0, z2_mx, cols)
        for m in range(1, PACK):
            product(b_ps[m][:], w2_mx, m, z2_mx, ALL)

        b7_last = keep.tile([P, S], F32, name="b7_last")
        b8, sum7, sum8, res = f32_tiles("b8_", S), f32_tiles("sum7_", S), f32_tiles("sum8_", S), f32_tiles("res", S)
        for h, cols in enumerate(HALVES):
            nc.vector.tensor_copy(b[0][:, cols], b0_ps[h][:])

        def add8(m):
            nc.vector.tensor_tensor(sum8[m][:], b8[m][:], a6[m][:], ALU.add)

        def finish(m, cols):
            nc.vector.tensor_tensor(res[m][:, cols], sum7[m][:, cols], sum8[m][:, cols], ALU.max)
            nc.sync.dma_start(out[m * P : (m + 1) * P, cols], res[m][:, cols])

        for m in range(last):
            nc.scalar.copy(b[m + 1][:, :S], b_ps[m + 1][:])
            nc.vector.tensor_tensor(sum7[m][:], b[m][:].indirect(l7[:]), a5[m][:], ALU.add)
            gather(b8[m][:], b[m], l8[:])
            if m > 0:
                add8(m - 1)
                finish(m - 1, ALL)
        gather(b8[last][:], b[last], l8[:])
        for cols, offsets in list_halves(l7):
            gather(b7_last[:, cols], b[last], offsets)
        add8(last - 1)
        finish(last - 1, ALL)
        add8(last)
        for cols in HALVES:
            nc.vector.tensor_tensor(sum7[last][:, cols], b7_last[:, cols], a5[last][:, cols], ALU.add)
        for cols in HALVES:
            finish(last, cols)
